import numpy as np, ml_dtypes
CORES = [66,74,82,90,194,202,210,218]
N = 8
BF = ml_dtypes.bfloat16
def gentries(a):
    return np.ascontiguousarray(a.reshape(8, 16, -1).transpose(0, 2, 1)).reshape(8, -1)
def gtable(e):
    e = np.asarray(e); return np.ascontiguousarray(e.reshape(8, -1, 16).transpose(0, 2, 1)).reshape(128, -1).astype(np.int32)
W, MA, J, P, T = 1792, 128, 384, 3, 3
def lanes(rng, big=False):
    jm = np.zeros((N, 8, MA), np.int64); lab = np.zeros((N, 8, J), np.int64); nx = np.zeros((N, 8, 16, J), np.int64)
    for q in range(N):
        for g in range(8):
            o = rng.permutation(J); p = rng.permutation(MA)
            tail = p[(MA * rng.random(J - MA) ** 2).astype(np.int64)]
            if big: tail[:] = p[0]
            lb = np.concatenate([np.arange(MA), tail]); s = np.argsort(lb, kind="stable"); cnt = np.bincount(lb, minlength=MA); st = np.add.accumulate(cnt) - cnt
            jm[q, g] = o[:MA]; lab[q, g, o] = lb
            nx[q, g][:, o] = o[s[st[lb] + (cnt[lb] * rng.random((16, J))).astype(np.int64)]]
            if big:
                pos = np.zeros(J, np.int64); pos[s] = np.arange(J) - st[lb[s]]
                nx[q, g][:8, o] = o[s[st[lb] + (pos + 1) % cnt[lb]]]
    return jm, lab, nx
def parts(rng, big=False):
    jm, lab, nx = lanes(rng, big); pal = rng.integers(0, W, (8, 16, MA, 6))
    ga = np.arange(8)[None, :, None, None]; ka = np.arange(16)[None, None, :, None]
    tool = np.where(rng.random((N, 8, 16, J)) < 0.75, pal[ga, ka, lab[:, :, None, :], rng.integers(0, 6, (N, 8, 16, J))], rng.integers(0, W, (N, 8, 16, J)))
    sh = (N, 8, 16, P, MA)
    name = np.where(rng.random(sh) < 0.8, pal[ga[..., None], ka[..., None], np.arange(MA), rng.integers(0, 6, sh)], rng.integers(0, W, sh))
    x = np.clip(rng.integers(0, 256, (N, 8, 1, W)) + rng.integers(-64, 65, (N, 8, 16, W)), 0, 255)
    lm = np.clip(rng.integers(64, 257, (N, 8, 1, J)) + rng.integers(-48, 49, (N, 8, 16, J)), 0, 255)
    return {"jm": jm, "nx": nx, "tool": tool, "name": name, "f": rng.integers(0, J, sh), "x": x, "lm": lm, "sd": rng.integers(0, 256, (N, 8, 16, W)), "rt": rng.integers(0, 65, (N, 8, 16, T))}
def full(a):
    return np.ascontiguousarray(a.reshape(N, 128, -1))
def pack(v):
    b = {k: full(v[k]).astype(np.float32).astype(BF) for k in ("x", "sd", "lm", "rt")}
    return {"xw": b["x"], "sd": b["sd"], "jt": full(4096 * v["nx"] + v["tool"]).astype(np.int32), "lm": b["lm"], "rt": b["rt"],
            "pk": full(4096 * v["f"] + v["name"]).astype(np.int32), "jm": np.stack([gtable(a) for a in v["jm"]])}
def setup_inputs(rng):
    return pack(parts(rng))
def setup_inputs_ties(rng):
    v = parts(rng)
    n = rng.choice(np.array([0, 7, 8, 9, 10, 16]), (N, 8, 1, W)); r = np.argsort(rng.random((N, 8, 16, W)), axis=2)
    v["x"] = 100 + (r < n).astype(np.int64); v["lm"] = np.full((N, 8, 16, J), 100); v["rt"] = rng.integers(0, 3, (N, 8, 16, T))
    v["f"] = rng.choice(np.array([0, J // 2, J - 1]), (N, 8, 16, P, MA))
    v["name"][:, :, :, 1] = np.where(rng.random((N, 8, 16, MA)) < 0.5, v["name"][:, :, :, 0], v["name"][:, :, :, 1])
    return pack(v)
def setup_inputs_crowd(rng):
    v = parts(rng); few = rng.integers(0, W, (8, 24)); ga = np.arange(8)[None, :, None, None]; m = np.arange(MA)
    v["tool"] = few[ga, rng.integers(0, 24, (N, 8, 16, J))]; v["name"] = few[ga[..., None], rng.integers(0, 24, (N, 8, 16, P, MA))]
    v["x"] = rng.choice(np.array([0, 3, 7, 8, 9, 128, 250, 254, 255]), (N, 8, 16, W)); v["rt"] = rng.choice(np.array([0, 1, 5, 64]), (N, 8, 16, T))
    other = np.setdiff1d(np.arange(W), few)
    for q in range(N):
        o = rng.permutation(8)
        g = o[0]; c, d = rng.permutation(other)[:2]
        v["lm"][q, g] = 255; v["tool"][q, g] = d; v["name"][q, g] = c; v["f"][q, g][:, 0] = J - 1; v["x"][q, g][:, c] = rng.integers(32, 256, 16)
        for g, w in ((o[1], 0), (o[2], 255)):
            c, d, e = rng.permutation(other)[:3]; m0 = int(rng.integers(1, 9))
            nm = np.where(m < m0, e, c); goes = (m == m0) == (w == 0)
            v["lm"][q, g] = 255; v["x"][q, g] = w; v["name"][q, g][0] = nm
            v["tool"][q, g][0, v["jm"][q, g]] = np.where(goes, nm, d)
            v["rt"][q, g] = rng.integers(17, 65, (16, T)) if w == 0 else rng.integers(0, 3, (16, T))
        g = o[3]; a = rng.permutation(W)[:17]; k0 = rng.integers(1, 8, MA)
        v["x"][q, g][:, a[0]] = rng.integers(0, 150, 16)
        v["x"][q, g][:, a[1:]] = rng.permuted(np.tile(rng.integers(150, 256, (16, 1)), (1, 16)), axis=0)
        v["tool"][q, g][:, v["jm"][q, g]] = np.where(np.arange(16)[:, None] < k0[None, :], a[0], a[1:][:, None])
    return pack(v)
def setup_inputs_ends(rng):
    v = parts(rng, True); e = np.array([0, 1, W - 2, W - 1])
    v["tool"] = np.where(rng.random((N, 8, 16, J)) < 0.5, rng.choice(e, (N, 8, 16, J)), v["tool"])
    v["name"] = np.where(rng.random((N, 8, 16, P, MA)) < 0.5, rng.choice(e, (N, 8, 16, P, MA)), v["name"])
    v["sd"] = np.where(rng.random((N, 8, 16, W)) < 0.5, rng.choice(np.array([0, 1, 255]), (N, 8, 16, W)), v["sd"])
    v["f"] = np.where(rng.random((N, 8, 16, P, MA)) < 0.5, rng.choice(np.array([0, J - 1]), (N, 8, 16, P, MA)), v["f"])
    return pack(v)
def setup_inputs_calm(rng):
    v = parts(rng); q = rng.permutation(N)
    v["lm"][q[0]] = 255; a = np.take_along_axis(v["tool"][q[0]], v["jm"][q[0]][:, None, :], 2)
    np.put_along_axis(v["name"][q[0]], rng.integers(0, P, (8, 16, 1, MA)), a[:, :, None, :], 2)
    v["lm"][q[1]] = 0; v["x"][q[1]] = np.maximum(v["x"][q[1]], 1)
    v["tool"][q[2]] = 2 * (v["tool"][q[2]] // 2); v["sd"][q[2]] = 2 * (v["sd"][q[2]] // 2); v["name"][q[2]] = 2 * (v["name"][q[2]] // 2) + 1
    return pack(v)
def setup_inputs_spread(rng):
    v = parts(rng)
    v["x"] = np.minimum((np.exp2(8 * rng.random((N, 8, 1, W))) * rng.random((N, 8, 16, W))).astype(np.int64), 255)
    v["lm"] = np.minimum((np.exp2(8 * rng.random((N, 8, 1, J))) * rng.random((N, 8, 16, J))).astype(np.int64), 255)
    v["rt"] = np.minimum(np.exp2(6 * rng.random((N, 8, 16, T))).astype(np.int64), 64)
    v["sd"] = np.minimum(np.exp2(8 * rng.random((N, 8, 16, W))).astype(np.int64), 255)
    v["tool"] = np.where(rng.random((N, 8, 16, J)) < 0.5, np.minimum((W * rng.random((N, 8, 16, J)) ** 3).astype(np.int64), W - 1), v["tool"])
    v["f"] = np.minimum((J * rng.random((N, 8, 16, P, MA)) ** 3).astype(np.int64), J - 1)
    return pack(v)
def check_inputs(d):
    bad = []
    for k, hi in (("xw", 255), ("sd", 255), ("lm", 255), ("rt", 64)):
        v = np.asarray(d[k]).astype(np.float64)
        if not np.all((v >= 0) & (v <= hi) & (v == np.floor(v))): bad.append("range of " + k)
    for k in ("jt", "pk"):
        v = np.asarray(d[k]).astype(np.int64)
        if np.min(v) < 0 or np.max(v) > 4096 * J - 1 or np.max(v & 4095) > W - 1: bad.append("range of " + k)
    if np.min(d["jm"]) < 0 or np.max(d["jm"]) > J - 1: bad.append("range of jm")
    if bad: return bad
    ok = True; nx = np.asarray(d["jt"]).astype(np.int64).reshape(N, 8, 16, J) >> 12
    for q in range(N):
        starts = gentries(np.asarray(d["jm"][q])).astype(np.int64)
        for g in range(8):
            fr = starts[g]; lab = np.full(J, -1)
            if len(np.unique(fr)) < MA: ok = False; continue
            lab[fr] = np.arange(MA)
            while len(fr):
                tg = nx[q, g][:, fr].reshape(-1); lb = np.tile(lab[fr], 16); new = lab[tg] < 0
                lab[tg[new]] = lb[new]
                if np.any(lab[tg] != lb): ok = False; break
                fr = np.unique(tg[new])
    if not ok: bad.append("lanes: a job can be reached from the starting jobs of two machines")
    return bad
def reference(xw, sd, jt, lm, rt, pk, jm):
    x = xw.astype(np.int64).reshape(N, 8, 16, W); s = sd.astype(np.int64).reshape(N, 8, 16, W); lim = lm.astype(np.int64).reshape(N, 8, 16, J); wr = rt.astype(np.int64).reshape(N, 8, 16, T)
    tab = jt.astype(np.int64).reshape(N, 8, 16, J); p = pk.astype(np.int64).reshape(N, 8, 16, P, MA)
    j = np.stack([gentries(a) for a in jm]).astype(np.int64)
    qa = np.arange(N)[:, None, None]; ga = np.arange(8)[None, :, None]
    for t in range(T):
        jj = np.ascontiguousarray(np.broadcast_to(j[:, :, None, :], (N, 8, 16, MA)))
        rec = np.take_along_axis(tab, jj, 3); a = rec & 4095; n = rec >> 12
        xa = np.take_along_axis(x, a.reshape(N, 8, 1, 16 * MA), 3).reshape(N, 8, 16, 16, MA)
        over = xa > np.take_along_axis(lim, jj, 3)[:, :, :, None, :]
        cond = np.add.reduce(over.astype(np.int64), axis=2) >= 9
        ks = np.argmax(np.add.reduce(xa, axis=2), axis=2)[:, :, None]
        b = a + np.take_along_axis(s, a, 3); b = np.where(b >= W, b - W, b)
        n2 = np.take_along_axis(tab, n, 3) >> 12
        a = np.where(cond, b, a); n = np.where(cond, n2, n)
        np.put_along_axis(tab, jj, 4096 * n + a, 3)
        eq = (p & 4095) == a[:, :, :, None]; hit = np.any(eq, axis=3)
        slot = np.where(hit, np.argmax(eq, axis=3), np.argmax(p >> 12, axis=3))[:, :, :, None]
        old = np.take_along_axis(p, slot, 3)[:, :, :, 0]
        send = np.where(hit, p[:, :, :, P - 1], old)
        np.put_along_axis(p, slot, (4096 * n + a)[:, :, :, None], 3)
        p[:, :, :, P - 1] = np.roll(send, 1, axis=0)
        v = np.take_along_axis(np.where(hit, a, old & 4095), ks, 2)[:, :, 0]; up = np.take_along_axis(hit, ks, 2)[:, :, 0]
        j = np.take_along_axis(n, ks, 2)[:, :, 0]
        low = np.full((N, 8, W), MA); np.minimum.at(low, (qa, ga, v), np.arange(MA)[None, None, :])
        wears = np.take_along_axis(up, np.minimum(low, MA - 1), 2)[:, :, None]
        x = np.where((low < MA)[:, :, None], np.where(wears, np.minimum(x + wr[:, :, :, t:t + 1], 255), np.maximum(x - 8, 0)), x)
    return {"yx": x.reshape(N, 128, W).astype(np.float32).astype(BF), "yp": p.reshape(N, 128, P * MA).astype(np.float32)}

@@ -1,0 +1,415 @@
+from concourse.mybir import AluOpType, AxisListType, ActivationFunctionType
+
+A = AluOpType
+CPY = ActivationFunctionType.Copy
+IDN = ActivationFunctionType.Identity
+W, MA, J, NT = 1792, 128, 384, 3
+XV = (64, 24, 24)
+
+_B, _H, _F, _I, _U = "bfloat16", "float16", "float32", "int32", "uint16"
+SCRATCH = {}
+for _names, _w, _d in (
+        ("sdt", W, _B), ("xt", W + MA, _B), ("lmt nxt", J, _B), ("rtb", NT, _B), ("rt8", NT, _F),
+        ("jtt pkt tint nint mall", J, _I), ("jmt kgi", 8, _I), ("tool", J, _F), ("jl vl ofl", 8 * NT, _U), ("al nl", 128, _U),
+        ("xa sg ng ov fd", 2048, _B), ("gm", 128, _B), ("af pre key uw um gout gsum msk rm land2", 128, _F),
+        ("lg nb cc nn nh e0 e1 e2 hit hh v0 v1 s0 s1 shf yy yc", 128, _B), ("uh omv vh dup", 128, _H),
+        ("q0 q1 q2 qv m0 m1 m2 mv give0 give1 give2 gcl gmm land0 land1 iot pmi", 128, _I),
+        ("dm vlf off rcf", 8, _F), ("yo ys", 256, _F), ("zer tri", 512, _B), ("rc", 8, _H), ("kg k15", 8, _U), ("e16", 8, _B),
+        ("ones idb idn id15 idn15 id05 id8k bt bo tie", 128, _B), ("idh id4k id2k c385 c769", 128, _H),
+        ("ep", 160, _B), ("eph", 160, _H), ("gs gsn", 1024, _H)):
+    for _n in _names.split():
+        SCRATCH[_n] = ("sbuf", [128, _w], _d)
+SCRATCH["jt8"] = ("sbuf", [8, 128], _B)
+for _k in range(8):
+    SCRATCH["ps%d" % _k] = ("psum", [128, 512], _F)
+SEMAPHORES = ["sv", "ss", "sp", "sg", "ljm", "ljt", "llm", "lpk", "lrt", "lxw", "lsd", "a0", "a1", "a2", "sent", "ox", "op", "oq"]
+MSK, NOIDX = 2047, 4188159
+
+
+def rank_program(g, core, T, topo):
+    rank = T.rank_of(core)
+    if rank is None:
+        return
+    nxt_core = T.cores[(rank + 1) % len(T.cores)]
+    prv_core = T.cores[(rank - 1) % len(T.cores)]
+    rid, pid = topo.addr(nxt_core, core)
+    mask = topo.mask(core, nxt_core)
+    nrec = len(topo.engines(prv_core, core))
+
+    ENG = {"v": g.vector, "s": g.scalar, "p": g.tensor, "g": g, "y": g.sync}
+    OWN = {"v": "sv", "s": "ss", "p": "sp", "g": "sg"}
+    cnt = {"sv": 0, "ss": 0, "sp": 0, "sg": 0}
+    clk = {e: {} for e in ENG}
+    snap = {}
+    wr, rd, bk = {}, {}, {}
+
+    def wait(e, toks):
+        for tk in sorted(toks, key=lambda q: (-len(snap[q]), q)):
+            sem, val = tk
+            if clk[e].get(sem, 0) >= val:
+                continue
+            if any(o != tk and snap[o].get(sem, 0) >= val and clk[e].get(o[0], 0) < o[1] for o in toks):
+                continue
+            ENG[e].wait_ge(T.sem[sem], val)
+            for a, b in snap[tk].items():
+                if clk[e].get(a, 0) < b:
+                    clk[e][a] = b
+
+    def deps(e, r, w, banks):
+        toks = set()
+        for k in r:
+            if k in wr:
+                toks.add(wr[k][1])
+        for k in w:
+            if k in wr:
+                toks.add(wr[k][1])
+            for e2, tk in rd.get(k, {}).items():
+                if e2 != e:
+                    toks.add(tk)
+        for b in banks:
+            for e2, tk in bk.get(b, {}).items():
+                if e2 != e:
+                    toks.add(tk)
+        if e == "p":
+            toks = {q for q in toks if q[0] != "sp"}
+        return toks
+
+    def note(e, tk, r, w, banks):
+        s = dict(clk[e])
+        if s.get(tk[0], 0) < tk[1]:
+            s[tk[0]] = tk[1]
+        snap[tk] = s
+        for k in w:
+            wr[k] = (e, tk)
+            rd[k] = {}
+        for k in r:
+            rd.setdefault(k, {})[e] = tk
+        for b in banks:
+            bk.setdefault(b, {})[e] = tk
+
+    def op(e, call, r=(), w=(), b=()):
+        wait(e, deps(e, r, w, b))
+        ins = call()
+        sem = OWN[e]
+        cnt[sem] += 1
+        ins.then_inc(T.sem[sem], 1)
+        note(e, (sem, cnt[sem]), r, w, b)
+
+    def dma(e, out, in_, sem, r=(), w=()):
+        wait(e, deps(e, r, w, ()))
+        ENG[e].dma_start(out, in_).then_inc(T.sem[sem], 16)
+        note(e, (sem, 16), r, w, ())
+
+    def res(x):
+        if isinstance(x, str):
+            return T[x][:, :], x, ()
+        if isinstance(x[0], int):
+            return T["ps%d" % x[0]][:, 128 * x[1]:128 * x[1] + 128], "ps%d_%d" % x, (x[0],)
+        return x[0], x[1], ()
+
+    def tt(out, a, b, o, extra=()):
+        (oa, ok, ob), (aa, ak, ab), (ba, bkk, bb) = res(out), res(a), res(b)
+        op("v", lambda: g.vector.tensor_tensor(oa, aa, ba, o), [ak, bkk] + list(extra), [ok], set(ob) | set(ab) | set(bb))
+
+    def ts(out, a, s1, s2, o0, o1=None, extra=()):
+        (oa, ok, ob), (aa, ak, ab) = res(out), res(a)
+        if o1 is None:
+            f = lambda: g.vector.tensor_scalar(oa, aa, s1, None, o0)
+        else:
+            f = lambda: g.vector.tensor_scalar(oa, aa, s1, s2, o0, o1)
+        op("v", f, [ak] + list(extra), [ok], set(ob) | set(ab))
+
+    def cp(out, a, extra=()):
+        (oa, ok, ob), (aa, ak, ab) = res(out), res(a)
+        op("v", lambda: g.vector.tensor_copy(oa, aa), [ak] + list(extra), [ok], set(ob) | set(ab))
+
+    def act(out, a, func=CPY, extra=(), **kw):
+        (oa, ok, ob), (aa, ak, ab) = res(out), res(a)
+        op("s", lambda: g.scalar.activation(oa, aa, func, **kw), [ak] + list(extra), [ok], set(ob) | set(ab))
+
+    def mm(out, l, r, st, sp):
+        (la, lk, _x), (ra, rk, _y) = res(l), res(r)
+        op("p", lambda: g.tensor.matmul(out[0], la, ra, st, sp), [lk, rk], [out[1]], (out[2],))
+
+    def P(p, a=0, b=128, step=1):
+        base = 128 * p[1]
+        return (T["ps%d" % p[0]][:, base + a:base + b:step], "ps%d_%d" % p, p[0])
+
+    def lst(nm, t):
+        return T[nm][:, 8 * t:8 * t + 8]
+
+    dma("y", T.jmt[:, :], T.jm[:, :], "ljm", w=["jmt"])
+    dma("s", T.jtt[:, :], T.jt[:, :], "ljt", w=["jtt"])
+    dma("y", T.xt[:, 0:W], T.xw[:, :], "lxw", w=["xt"])
+    dma("y", T.pkt[:, :], T.pk[:, :], "lpk", w=["pkt"])
+    dma("y", T.lmt[:, :], T.lm[:, :], "llm", w=["lmt"])
+    dma("s", T.sdt[:, :], T.sd[:, :], "lsd", w=["sdt"])
+    dma("y", T.rtb[:, :], T.rt[:, :], "lrt", w=["rtb"])
+
+    def fill(ap, key, c):
+        op("v", lambda: g.vector.memset(ap, c), (), [key])
+
+    def asel(out, in_, pat, cmp_, f, base, cm):
+        op("g", lambda: g.affine_select(T[out][:, :], T[in_][:, :], pat, cmp_, f, base, cm), [in_], [out])
+
+    fill(T.ones[:, :], "ones", 1.0)
+    fill(T.zer[:, :], "zer", 0.0)
+    asel("idb", "ones", [[-1, 128]], A.is_equal, 0.0, 0, 1)
+    asel("bt", "ones", [[-16, 8], [0, 16]], A.is_ge, 0.0, 0, 1)
+    asel("bo", "bt", [[16, 8], [0, 16]], A.is_ge, 0.0, 15, -1)
+    op("g", lambda: g.iota(T.tie[:, :], [[0, 8], [-1, 16]], 15, 0, allow_small_or_imprecise_dtypes=True), (), ["tie"])
+    op("g", lambda: g.iota(T.kgi[:, :], [[1, 8]], 0, 0), (), ["kgi"])
+    op("g", lambda: g.iota(T.iot[:, :], [[-1, 128]], 128, 1), (), ["iot"])
+    op("g", lambda: g.iota(T.rcf[:, :], [[0, 8]], 1792, 1, allow_small_or_imprecise_dtypes=True), (), ["rcf"])
+    asel("tri", "zer", [[0, 4], [-1, 128]], A.is_ge, 4096.0, -1, 1)
+    fill(T.fd[:, :], "fd", 0.0)
+    fill(T.ep[:, :], "ep", 0.0)
+    for k in range(16):
+        op("v", lambda: g.vector.tensor_copy(T.fd[:, 129 * k:128 * k + 128:16], T.idb[:, k:128:16]), ["idb"] + (["fd"] if k == 0 else []), ["fd%d" % k])
+    for nm, c in (("idn", -1.0), ("id15", 1.5), ("idn15", -1.5), ("id05", 0.5), ("id8k", 8192.0)):
+        act(nm, "idb", scale=c)
+
+    op("v", lambda: g.vector.tensor_copy(lst("jl", 0), T.jmt[:, :]), ["jmt"], ["jl0"])
+    ts("nint", "jtt", 12, None, A.logical_shift_right)
+    ts("tint", "jtt", 4095, None, A.bitwise_and)
+    ts("nxt", "nint", -192.0, None, A.add)
+    cp("tool", "tint")
+
+    def nexts(h):
+        act((T.ng[:, 1024 * h:1024 * h + 1024], "ng%d" % h), (T.nxt[:, :].indirect(T.nl[:, 64 * h:64 * h + 64]), "nxt"), extra=["nl"])
+
+    def limits(t):
+        act("lg", (T.lmt[:, :].indirect(lst("jl", t)), "lmt"), extra=["jl%d" % t])
+
+    def next_lists(t):
+        jk, jl = "jl%d" % t, lst("jl", t)
+        act("nb", (T.nxt[:, :].indirect(jl), "nxt"), extra=[jk])
+        ts("nl", (T.nxt[:, :].indirect(jl), "nxt"), 192.0, None, A.add, extra=[jk])
+        nexts(0)
+
+    def tool_lists(t):
+        jk, jl = "jl%d" % t, lst("jl", t)
+        cp("al", (T.tool[:, :].indirect(jl), "tool"), extra=[jk])
+        act("af", (T.tool[:, :].indirect(jl), "tool"), extra=[jk])
+
+    def diag(src, piece, first):
+        for h in range(2):
+            o = P(piece, 64 * h, 64 * h + 64)
+            if first:
+                mm(o, "idn", (T.nb[:, 64 * h:64 * h + 64], "nb"), True, False)
+            for k in range(16):
+                mm(o, (T.fd[:, 128 * k:128 * k + 128], "fd%d" % k), (T[src][:, 1024 * h + k:1024 * h + 1024:16], "%s%d" % (src, h)),
+                   k == 0 and not first, k == 15)
+            yield h
+
+    next_lists(0)
+    nexts(1)
+    limits(0)
+    tool_lists(0)
+    op("v", lambda: g.vector.tensor_copy(T.ep[:, 16:144:16], T.bo[:, 0:128:16]), ["bo"], ["ep"])
+    op("v", lambda: g.vector.tensor_scalar(T.e16[:, :], T.bo[:, 0:128:16], 16.0, None, A.mult), ["bo"], ["e16"])
+    ts("msk", "tie", 15.0, None, A.is_lt)
+    op("v", lambda: g.vector.tensor_scalar(T.k15[:, :], T.kgi[:, :], 16.0, 15.0, A.mult, A.add), ["kgi"], ["k15"])
+    for q in range(8):
+        op("v", lambda: g.vector.tensor_scalar(T.gs[:, 128 * q:128 * q + 128], T.ones[:, :], T.bo[:, 16 * q:16 * q + 1], None, A.mult), ["ones", "bo"], ["gs"] if q == 7 else ["gs_%d" % q])
+    ts("gsn", "gs", -1.0, None, A.mult, extra=["gs_%d" % q for q in range(7)])
+    cp("idh", "idb")
+    cp("eph", "ep")
+    ts("id4k", "idb", 4096.0, None, A.mult)
+    ts("id2k", "idb", 2048.0, None, A.mult)
+    ts("c385", "ones", 385.0, None, A.mult)
+    ts("c769", "ones", 769.0, None, A.mult)
+    ts("pmi", "iot", 15, None, A.bitwise_and)
+    op("v", lambda: g.vector.tensor_tensor(T.rc[:, :], T.rcf[:, :], T.bo[:, 0:128:16], A.mult), ["rcf", "bo"], ["rc"])
+    cp("kg", "kgi")
+    ts("rm", "pmi", 0.0, -1.0, A.is_equal, A.add)
+
+    MN = [(T.mall[:, 0:128], "mall"), (T.mall[:, 128:256], "mall"), (T.mall[:, 256:384], "mall")]
+
+    def first_pockets():
+        ts("mall", "pkt", 4095, None, A.bitwise_and)
+        for i in range(3):
+            ts((0, i), (T.pkt[:, 128 * i:128 * i + 128], "pkt"), 2.0, 2048.0 * (2 - i), A.mult, A.add)
+        for i in range(3):
+            tt("q%d" % i, (0, i), MN[i], A.subtract)
+        tt((0, 0), "q0", "q1", A.max)
+
+    late = [first_pockets]
+
+    for t in range(NT):
+        last = t == NT - 1
+        jk, jl = "jl%d" % t, lst("jl", t)
+        for h in diag("ng", (4, 0), True):
+            pass
+        mm(P((4, 1)), "idb", "lg", True, True)
+        xv = XV[t]
+        op("v", lambda: g.vector.tensor_copy(T.xa[:, 0:16 * xv], T.xt[:, 0:W].indirect(T.al[:, 0:xv])), ["xt", "al"], ["xa0"])
+        op("s", lambda: g.scalar.activation(T.xa[:, 16 * xv:2048], T.xt[:, 0:W].indirect(T.al[:, xv:128]), CPY), ["xt", "al"], ["xa1"])
+        for h in range(2):
+            act((T.sg[:, 1024 * h:1024 * h + 1024], "sg%d" % h), (T.sdt[:, :].indirect(T.al[:, 64 * h:64 * h + 64]), "sdt"), extra=["al"])
+        for b in range(2):
+            mm((T["ps%d" % (6 + b)][:, :], "ps%d" % (6 + b), 6 + b), "idb", "tri", True, False)
+        mm(P((1, 0)), "idb", "tie", True, False)
+        for k in range(16):
+            o = P((1, 0), k, 128, 16)
+            op("p", lambda: g.tensor.matmul(o[0], T.xa[:, k:2048:16], T.e16[:, :], False, k == 15), ["xa0", "xa1", "e16"], [o[1]], (1,))
+        late[-1]()
+        if t > 0:
+            ld = "land%d" % (t - 1)
+            tk = ("a%d" % (t - 1), nrec)
+            snap[tk] = {tk[0]: nrec}
+            wr[ld] = ("r", tk)
+            ts("q2", ld, NOIDX, None, A.bitwise_and)
+            ts("m2", ld, MSK, None, A.bitwise_and)
+            MN[2] = "m2"
+        else:
+            ts("rt8", "rtb", 8.0, None, A.add)
+        tt("qv", (0, 0), "q2", A.max)
+        tt((0, 1), (0, 0), "q2", A.max)
+        ts("mv", "qv", MSK, None, A.bitwise_and)
+        tt("v0", "q0", (0, 1), A.is_equal)
+        tt("v1", "q1", (0, 1), A.is_equal)
+        tt((0, 2), "q2", (0, 1), A.subtract)
+
+        def compare(k):
+            op("v", lambda: g.vector.tensor_tensor(T.ov[:, 128 * k:128 * k + 128], T.xa[:, k:2048:16], T.ps4[:, 128:256], A.is_gt),
+               ["xa0", "xa1", "ps4_1"], ["ov%d" % k], (4,))
+            mm(P((2, 0)), (T.ep[:, 16 - k:144 - k], "ep"), (T.ov[:, 128 * k:128 * k + 128], "ov%d" % k), k == 0, k == 15)
+
+        compare(0)
+        compare(1)
+        op("v", lambda: g.vector.tensor_tensor_scan(T.pre[:, :], T.msk[:, :], T.ps1[:, 0:128], 0.0, A.mult, A.max), ["msk", "ps1_0"], ["pre"], (1,))
+        cp("key", (1, 0))
+        compare(2)
+        tt("gm", (T.pre[:, :].indirect(T.k15[:, :]), "pre"), "key", A.is_equal, extra=["k15"])
+        for k in range(3, 12):
+            compare(k)
+        mm(P((1, 1)), "gm", "idb", True, True)
+        for k in range(12, 16):
+            compare(k)
+        ts("cc", (2, 0), 9.0, None, A.is_ge)
+        tt((4, 2), "cc", (4, 0), A.mult)
+        tt("omv", "mv", (1, 1), A.mult)
+        tt("nn", "nb", (4, 2), A.add)
+        dg = diag("sg", (3, 0), False)
+        if not last:
+            tt("nh", "nn", (1, 1), A.mult)
+            for r in range(16):
+                mm((T.ps2[0:8, 128 + r:256:16], "ps2_1", 2), (T.nh[:, r:128:16], "nh"), (T.bo[:, 0:128:16], "bo"), True, True)
+            op("v", lambda: g.vector.tensor_copy(T.nxt[:, :].indirect(jl), T.nn[:, :]), ["nn", jk], ["nxt"])
+            op("v", lambda: g.vector.tensor_copy(T.jt8[:, :], T.ps2[0:8, 128:256]), ["ps2_1"], ["jt8"], (2,))
+        next(dg)
+        if not last:
+            mm(P((2, 2), 0, 8), "jt8", (T.idb[0:8, 0:8], "idb"), True, True)
+        next(dg)
+        if not last:
+            op("v", lambda: g.vector.tensor_scalar(lst("jl", t + 1), T.ps2[:, 256:264], 192.0, None, A.add), ["ps2_2"], ["jl%d" % (t + 1)], (2,))
+            limits(t + 1)
+            next_lists(t + 1)
+        tt((3, 1), "cc", (3, 0), A.mult)
+        tt("uw", "af", (3, 1), A.add)
+        ts((3, 2), "uw", 1792.0, -1792.0, A.is_ge, A.mult)
+        tt((3, 3), "uw", (3, 2), A.add)
+        tt("uh", "uw", (3, 2), A.add)
+        tt("e0", MN[0], (3, 3), A.is_equal)
+        tt("e1", MN[1], (3, 3), A.is_equal)
+        tt("e2", MN[2], (3, 3), A.is_equal)
+        o = P((5, 0))
+        mm(o, "idb", "e0", True, False)
+        mm(o, "idb", "e1", False, False)
+        mm(o, "idb", "e2", False, True)
+        tt("um", "mv", (3, 3), A.subtract)
+        tt((3, 1), "um", (1, 1), A.mult)
+        ts("hit", (5, 0), 1.0, None, A.min)
+        tt((3, 2), "hit", (3, 1), A.mult)
+        tt("vh", "omv", (3, 2), A.subtract)
+        tt("hh", "hit", (1, 1), A.mult)
+        o = P((5, 1))
+        mm(o, "id15", "e0", True, False)
+        mm(o, "id05", "v0", False, True)
+        o = P((5, 2))
+        mm(o, "id15", "e1", True, False)
+        mm(o, "idn15", "e0", False, False)
+        mm(o, "id05", "v1", False, True)
+        for b in range(2):
+            full = (T["ps%d" % (6 + b)][:, :], "ps%d" % (6 + b), 6 + b)
+            for q in range(4):
+                gg = 4 * b + q
+                mm((T["ps%d" % (6 + b)][:, 128 * q:128 * q + 128], "ps%d" % (6 + b), 6 + b), (T.gs[:, 128 * gg:128 * gg + 128], "gs"), "vh", False, False)
+            mm(full, "vh", (T.gsn[:, 512 * b:512 * b + 512], "gsn"), False, True)
+            if b == 0:
+                mm(P((2, 2)), "bo", "hh", True, True)
+        o = P((1, 2), 0, 8)
+        for r in range(16):
+            mm(o, (T.eph[:, 16 - r:144 - r], "eph"), (T.vh[:, r:128:16], "vh"), r == 0, r == 15)
+        for i in range(2):
+            o = P((4, 2 + i))
+            mm(o, "id8k", "nn", True, False)
+            mm(o, "idh", "uh", False, False)
+            mm(o, ("id4k", "id2k")[i], ("c385", "c769")[i], False, True)
+
+        def pockets(last=last):
+            tt("s0", "hit", (5, 1), A.is_lt)
+            tt("s1", "hit", (5, 2), A.is_lt)
+            tt((0, 0), "q0", (4, 2), A.subtract)
+            tt((0, 1), "q1", (4, 3), A.subtract)
+            tt((0, 0), "s0", (0, 0), A.mult)
+            tt((0, 1), "s1", (0, 1), A.mult)
+            tt("q0", "q0", (0, 0), A.subtract)
+            tt("q1", "q1", (0, 1), A.subtract)
+            ts("m0", "q0", MSK, None, A.bitwise_and)
+            ts("m1", "q1", MSK, None, A.bitwise_and)
+            MN[0], MN[1] = "m0", "m1"
+            if not last:
+                tt((0, 0), "q0", "q1", A.max)
+
+        late.append(pockets)
+
+        act("shf", (2, 2), IDN, extra=["rt8"], scale=T.rt8[:, t:t + 1], bias=-8.0)
+        gv = "give%d" % t
+        if not last:
+            nexts(1)
+            op("v", lambda: g.vector.tensor_copy(T.tool[:, :].indirect(jl), T.uh[:, :]), ["uh", jk], ["tool"])
+        tt((0, 3), "hit", (0, 2), A.mult)
+        tt(gv, "qv", (0, 3), A.add)
+        if not last:
+            tool_lists(t + 1)
+            out = gv
+        else:
+            ts("gcl", gv, NOIDX, None, A.bitwise_and)
+            ts("gmm", gv, MSK, None, A.bitwise_and)
+            tt("gsum", "gcl", "gmm", A.add)
+            ts("gout", "gsum", 0.5, None, A.mult)
+            out = "gout"
+        wait("g", deps("g", [out], (), ()))
+        g.remote_dma(T["land%d" % t][:, :], T[out][:, :], T.sem["a%d" % t], T.sem.sent, pid, rid, mask)
+        for gg in range(8):
+            b, q = 6 + gg // 4, gg % 4
+            op("v", lambda: g.vector.tensor_reduce(T.dm[:, gg:gg + 1], T["ps%d" % b][:, 128 * q:128 * q + 128], AxisListType.X, A.min, apply_absolute_value=True),
+               ["ps%d" % b], ["dm%d" % gg], (b,))
+        vk, ok_ = "vl%d" % t, "ofl%d" % t
+        dmk = ["dm%d" % q for q in range(8)]
+        op("v", lambda: g.vector.tensor_tensor(T.dup[:, :], T.dm[:, :].indirect(T.kg[:, :]), T.rm[:, :], A.is_equal), dmk + ["kg", "rm"], ["dup"])
+        op("v", lambda: g.vector.tensor_copy(lst("vl", t), T.ps1[:, 256:264]), ["ps1_2"], [vk], (1,))
+        op("v", lambda: g.vector.tensor_copy(T.vlf[:, :], T.ps1[:, 256:264]), ["ps1_2"], ["vlf"], (1,))
+        mm((T.ps2[:, 384:392], "ps2_3", 2), "dup", "rc", True, True)
+        tt("yy", (T.xt[:, 0:W].indirect(lst("vl", t)), "xt"), "shf", A.add, extra=[vk])
+        op("v", lambda: g.vector.tensor_tensor(T.off[:, :], T.vlf[:, :], T.ps2[:, 384:392], A.max), ["vlf", "ps2_3"], ["off"], (2,))
+        ts("yc", "yy", 0.0, 255.0, A.max, A.min)
+        op("v", lambda: g.vector.tensor_copy(lst("ofl", t), T.off[:, :]), ["off"], [ok_])
+        op("v", lambda: g.vector.tensor_copy(T.xt[:, :].indirect(lst("ofl", t)), T.yc[:, :]), ["yc", ok_], ["xt"])
+        if last:
+            dma("y", T.yx[:, :], T.xt[:, 0:W], "ox", r=["xt"])
+            pockets()
+            for i in range(2):
+                tt((T.ys[:, 128 * i:128 * i + 128], "ys%d" % i), "q%d" % i, "m%d" % i, A.add)
+            for i in range(2):
+                ts((T.yo[:, 128 * i:128 * i + 128], "yo%d" % i), (T.ys[:, 128 * i:128 * i + 128], "ys%d" % i), 0.5, -1024.0 * (2 - i), A.mult, A.add)
+            dma("s", T.yp[:, 0:256], T.yo[:, :], "op", r=["yo0", "yo1"])
+    g.scalar.wait_ge(T.sem.a2, nrec)
+    g.scalar.dma_start(T.yp[:, 256:384], T.land2[:, :]).then_inc(T.sem.oq, 16)
+    for sem in ("sv", "ss", "sp", "sg"):
+        g.wait_ge(T.sem[sem], cnt[sem])
+    g.wait_ge(T.sem.sent, NT * len(topo.engines(core, nxt_core)))
+    for sem in ("ox", "op", "oq"):
+        g.wait_ge(T.sem[sem], 16)

@@ -4,7 +4,8 @@ A = AluOpType
 CPY = ActivationFunctionType.Copy
 IDN = ActivationFunctionType.Identity
 W, MA, J, NT = 1792, 128, 384, 3
-XV = (64, 24, 24)
+XV = (112, 40, 40)
+C1 = 8
 
 _B, _H, _F, _I, _U = "bfloat16", "float16", "float32", "int32", "uint16"
 SCRATCH = {}
@@ -15,7 +16,7 @@ for _names, _w, _d in (
         ("lg nb cc nn nh e0 e1 e2 hit hh v0 v1 s0 s1 shf yy yc", 128, _B), ("uh omv vh dup", 128, _H),
         ("q0 q1 q2 qv m0 m1 m2 mv give0 give1 give2 gcl gmm land0 land1 iot pmi", 128, _I),
         ("dm vlf off rcf", 8, _F), ("yo ys", 256, _F), ("zer tri", 512, _B), ("rc", 8, _H), ("kg k15", 8, _U), ("e16", 8, _B),
-        ("ones idb idn id15 idn15 id05 id8k bt bo tie", 128, _B), ("idh id4k id2k c385 c769", 128, _H),
+        ("ones id4m idn4m idb idn id15 idn15 id05 id8k bt bo tie", 128, _B), ("idh id4k id2k c385 c769", 128, _H),
         ("ep", 160, _B), ("eph", 160, _H), ("gs gsn", 1024, _H)):
     for _n in _names.split():
         SCRATCH[_n] = ("sbuf", [128, _w], _d)
@@ -141,10 +142,10 @@ def rank_program(g, core, T, topo):
     dma("y", T.jmt[:, :], T.jm[:, :], "ljm", w=["jmt"])
     dma("s", T.jtt[:, :], T.jt[:, :], "ljt", w=["jtt"])
     dma("y", T.xt[:, 0:W], T.xw[:, :], "lxw", w=["xt"])
-    dma("y", T.pkt[:, :], T.pk[:, :], "lpk", w=["pkt"])
     dma("y", T.lmt[:, :], T.lm[:, :], "llm", w=["lmt"])
     dma("s", T.sdt[:, :], T.sd[:, :], "lsd", w=["sdt"])
     dma("y", T.rtb[:, :], T.rt[:, :], "lrt", w=["rtb"])
+    dma("y", T.pkt[:, :], T.pk[:, :], "lpk", w=["pkt"])
 
     def fill(ap, key, c):
         op("v", lambda: g.vector.memset(ap, c), (), [key])
@@ -154,20 +155,28 @@ def rank_program(g, core, T, topo):
 
     fill(T.ones[:, :], "ones", 1.0)
     fill(T.zer[:, :], "zer", 0.0)
-    asel("idb", "ones", [[-1, 128]], A.is_equal, 0.0, 0, 1)
+    fill(T.fd[:, :], "fd", 0.0)
     asel("bt", "ones", [[-16, 8], [0, 16]], A.is_ge, 0.0, 0, 1)
     asel("bo", "bt", [[16, 8], [0, 16]], A.is_ge, 0.0, 15, -1)
+    asel("idb", "ones", [[-1, 128]], A.is_equal, 0.0, 0, 1)
     op("g", lambda: g.iota(T.tie[:, :], [[0, 8], [-1, 16]], 15, 0, allow_small_or_imprecise_dtypes=True), (), ["tie"])
     op("g", lambda: g.iota(T.kgi[:, :], [[1, 8]], 0, 0), (), ["kgi"])
     op("g", lambda: g.iota(T.iot[:, :], [[-1, 128]], 128, 1), (), ["iot"])
     op("g", lambda: g.iota(T.rcf[:, :], [[0, 8]], 1792, 1, allow_small_or_imprecise_dtypes=True), (), ["rcf"])
     asel("tri", "zer", [[0, 4], [-1, 128]], A.is_ge, 4096.0, -1, 1)
-    fill(T.fd[:, :], "fd", 0.0)
     fill(T.ep[:, :], "ep", 0.0)
     for k in range(16):
-        op("v", lambda: g.vector.tensor_copy(T.fd[:, 129 * k:128 * k + 128:16], T.idb[:, k:128:16]), ["idb"] + (["fd"] if k == 0 else []), ["fd%d" % k])
-    for nm, c in (("idn", -1.0), ("id15", 1.5), ("idn15", -1.5), ("id05", 0.5), ("id8k", 8192.0)):
+        op("s", lambda: g.scalar.activation(T.fd[:, 129 * k:128 * k + 128:16], T.idb[:, k:128:16], CPY), ["idb"] + (["fd"] if k == 0 else []), ["fd%d" % k])
+    for nm, c in (("idn", -1.0), ("id15", 1.5), ("idn15", -1.5), ("id05", 0.5), ("id8k", 8192.0), ("id4m", 4194304.0), ("idn4m", -4194304.0)):
         act(nm, "idb", scale=c)
+    ts("c385", "ones", 385.0, None, A.mult)
+    ts("c769", "ones", 769.0, None, A.mult)
+    op("v", lambda: g.vector.tensor_copy(T.ep[:, 16:144:16], T.bo[:, 0:128:16]), ["bo"], ["ep"])
+    op("v", lambda: g.vector.tensor_scalar(T.e16[:, :], T.bo[:, 0:128:16], 16.0, None, A.mult), ["bo"], ["e16"])
+    for q in range(8):
+        op("v", lambda: g.vector.tensor_scalar(T.gs[:, 128 * q:128 * q + 128], T.ones[:, :], T.bo[:, 16 * q:16 * q + 1], None, A.mult), ["ones", "bo"], ["gs"] if q == 7 else ["gs_%d" % q])
+    ts("msk", "tie", 15.0, None, A.is_lt)
+    op("v", lambda: g.vector.tensor_scalar(T.k15[:, :], T.kgi[:, :], 16.0, 15.0, A.mult, A.add), ["kgi"], ["k15"])
 
     op("v", lambda: g.vector.tensor_copy(lst("jl", 0), T.jmt[:, :]), ["jmt"], ["jl0"])
     ts("nint", "jtt", 12, None, A.logical_shift_right)
@@ -178,13 +187,13 @@ def rank_program(g, core, T, topo):
     def nexts(h):
         act((T.ng[:, 1024 * h:1024 * h + 1024], "ng%d" % h), (T.nxt[:, :].indirect(T.nl[:, 64 * h:64 * h + 64]), "nxt"), extra=["nl"])
 
-    def limits(t):
-        act("lg", (T.lmt[:, :].indirect(lst("jl", t)), "lmt"), extra=["jl%d" % t])
+    def sisters(h):
+        act((T.sg[:, 1024 * h:1024 * h + 1024], "sg%d" % h), (T.sdt[:, :].indirect(T.al[:, 64 * h:64 * h + 64]), "sdt"), extra=["al"])
 
     def next_lists(t):
         jk, jl = "jl%d" % t, lst("jl", t)
-        act("nb", (T.nxt[:, :].indirect(jl), "nxt"), extra=[jk])
         ts("nl", (T.nxt[:, :].indirect(jl), "nxt"), 192.0, None, A.add, extra=[jk])
+        act("nb", (T.nxt[:, :].indirect(jl), "nxt"), extra=[jk])
         nexts(0)
 
     def tool_lists(t):
@@ -192,33 +201,26 @@ def rank_program(g, core, T, topo):
         cp("al", (T.tool[:, :].indirect(jl), "tool"), extra=[jk])
         act("af", (T.tool[:, :].indirect(jl), "tool"), extra=[jk])
 
-    def diag(src, piece, first):
-        for h in range(2):
-            o = P(piece, 64 * h, 64 * h + 64)
-            if first:
-                mm(o, "idn", (T.nb[:, 64 * h:64 * h + 64], "nb"), True, False)
-            for k in range(16):
-                mm(o, (T.fd[:, 128 * k:128 * k + 128], "fd%d" % k), (T[src][:, 1024 * h + k:1024 * h + 1024:16], "%s%d" % (src, h)),
-                   k == 0 and not first, k == 15)
-            yield h
+    def limits(t):
+        act("lg", (T.lmt[:, :].indirect(lst("jl", t)), "lmt"), extra=["jl%d" % t])
+
+    def pick(src, piece, h, first):
+        o = P(piece, 64 * h, 64 * h + 64)
+        if first:
+            mm(o, "idn", (T.nb[:, 64 * h:64 * h + 64], "nb"), True, False)
+        for k in range(16):
+            mm(o, (T.fd[:, 128 * k:128 * k + 128], "fd%d" % k), (T[src][:, 1024 * h + k:1024 * h + 1024:16], "%s%d" % (src, h)),
+               k == 0 and not first, k == 15)
 
     next_lists(0)
+    tool_lists(0)
     nexts(1)
     limits(0)
-    tool_lists(0)
-    op("v", lambda: g.vector.tensor_copy(T.ep[:, 16:144:16], T.bo[:, 0:128:16]), ["bo"], ["ep"])
-    op("v", lambda: g.vector.tensor_scalar(T.e16[:, :], T.bo[:, 0:128:16], 16.0, None, A.mult), ["bo"], ["e16"])
-    ts("msk", "tie", 15.0, None, A.is_lt)
-    op("v", lambda: g.vector.tensor_scalar(T.k15[:, :], T.kgi[:, :], 16.0, 15.0, A.mult, A.add), ["kgi"], ["k15"])
-    for q in range(8):
-        op("v", lambda: g.vector.tensor_scalar(T.gs[:, 128 * q:128 * q + 128], T.ones[:, :], T.bo[:, 16 * q:16 * q + 1], None, A.mult), ["ones", "bo"], ["gs"] if q == 7 else ["gs_%d" % q])
     ts("gsn", "gs", -1.0, None, A.mult, extra=["gs_%d" % q for q in range(7)])
     cp("idh", "idb")
     cp("eph", "ep")
     ts("id4k", "idb", 4096.0, None, A.mult)
     ts("id2k", "idb", 2048.0, None, A.mult)
-    ts("c385", "ones", 385.0, None, A.mult)
-    ts("c769", "ones", 769.0, None, A.mult)
     ts("pmi", "iot", 15, None, A.bitwise_and)
     op("v", lambda: g.vector.tensor_tensor(T.rc[:, :], T.rcf[:, :], T.bo[:, 0:128:16], A.mult), ["rcf", "bo"], ["rc"])
     cp("kg", "kgi")
@@ -234,96 +236,127 @@ def rank_program(g, core, T, topo):
             tt("q%d" % i, (0, i), MN[i], A.subtract)
         tt((0, 0), "q0", "q1", A.max)
 
-    late = [first_pockets]
-
     for t in range(NT):
         last = t == NT - 1
         jk, jl = "jl%d" % t, lst("jl", t)
-        for h in diag("ng", (4, 0), True):
-            pass
-        mm(P((4, 1)), "idb", "lg", True, True)
         xv = XV[t]
+        if t:
+            sisters(0)
         op("v", lambda: g.vector.tensor_copy(T.xa[:, 0:16 * xv], T.xt[:, 0:W].indirect(T.al[:, 0:xv])), ["xt", "al"], ["xa0"])
         op("s", lambda: g.scalar.activation(T.xa[:, 16 * xv:2048], T.xt[:, 0:W].indirect(T.al[:, xv:128]), CPY), ["xt", "al"], ["xa1"])
-        for h in range(2):
-            act((T.sg[:, 1024 * h:1024 * h + 1024], "sg%d" % h), (T.sdt[:, :].indirect(T.al[:, 64 * h:64 * h + 64]), "sdt"), extra=["al"])
+        if t == 0:
+            sisters(0)
+        sisters(1)
+        pick("ng", (4, 0), 0, True)
+        pick("ng", (4, 0), 1, True)
+        mm(P((4, 1)), "idb", "lg", True, True)
+        if t:
+            pick("sg", (3, 0), 0, False)
         for b in range(2):
             mm((T["ps%d" % (6 + b)][:, :], "ps%d" % (6 + b), 6 + b), "idb", "tri", True, False)
         mm(P((1, 0)), "idb", "tie", True, False)
         for k in range(16):
             o = P((1, 0), k, 128, 16)
             op("p", lambda: g.tensor.matmul(o[0], T.xa[:, k:2048:16], T.e16[:, :], False, k == 15), ["xa0", "xa1", "e16"], [o[1]], (1,))
-        late[-1]()
-        if t > 0:
-            ld = "land%d" % (t - 1)
-            tk = ("a%d" % (t - 1), nrec)
-            snap[tk] = {tk[0]: nrec}
-            wr[ld] = ("r", tk)
-            ts("q2", ld, NOIDX, None, A.bitwise_and)
-            ts("m2", ld, MSK, None, A.bitwise_and)
-            MN[2] = "m2"
-        else:
-            ts("rt8", "rtb", 8.0, None, A.add)
-        tt("qv", (0, 0), "q2", A.max)
-        tt((0, 1), (0, 0), "q2", A.max)
-        ts("mv", "qv", MSK, None, A.bitwise_and)
-        tt("v0", "q0", (0, 1), A.is_equal)
-        tt("v1", "q1", (0, 1), A.is_equal)
-        tt((0, 2), "q2", (0, 1), A.subtract)
+
+        def beginning():
+            if t == 0:
+                first_pockets()
+                ts("rt8", "rtb", 8.0, None, A.add)
+            else:
+                tt("q0", "q0", (0, 0), A.subtract)
+                tt("q1", "q1", (0, 1), A.subtract)
+                ld = "land%d" % (t - 1)
+                tk = ("a%d" % (t - 1), nrec)
+                snap[tk] = {tk[0]: nrec}
+                wr[ld] = ("r", tk)
+                ts("m0", "q0", MSK, None, A.bitwise_and)
+                ts("m1", "q1", MSK, None, A.bitwise_and)
+                tt((0, 0), "q0", "q1", A.max)
+                ts("q2", ld, NOIDX, None, A.bitwise_and)
+                MN[0], MN[1], MN[2] = "m0", "m1", "m2"
+                ts("m2", ld, MSK, None, A.bitwise_and)
+            tt((0, 1), (0, 0), "q2", A.max)
+            tt("qv", (0, 0), "q2", A.max)
+            tt("v0", "q0", (0, 1), A.is_equal)
+            ts("mv", "qv", MSK, None, A.bitwise_and)
+
+        if t:
+            beginning()
 
         def compare(k):
             op("v", lambda: g.vector.tensor_tensor(T.ov[:, 128 * k:128 * k + 128], T.xa[:, k:2048:16], T.ps4[:, 128:256], A.is_gt),
                ["xa0", "xa1", "ps4_1"], ["ov%d" % k], (4,))
             mm(P((2, 0)), (T.ep[:, 16 - k:144 - k], "ep"), (T.ov[:, 128 * k:128 * k + 128], "ov%d" % k), k == 0, k == 15)
 
-        compare(0)
-        compare(1)
+        for k in range(C1):
+            compare(k)
         op("v", lambda: g.vector.tensor_tensor_scan(T.pre[:, :], T.msk[:, :], T.ps1[:, 0:128], 0.0, A.mult, A.max), ["msk", "ps1_0"], ["pre"], (1,))
         cp("key", (1, 0))
-        compare(2)
+        compare(C1)
+        compare(C1 + 1)
         tt("gm", (T.pre[:, :].indirect(T.k15[:, :]), "pre"), "key", A.is_equal, extra=["k15"])
-        for k in range(3, 12):
+        for k in range(C1 + 2, 12):
             compare(k)
+        if t == 0:
+            beginning()
         mm(P((1, 1)), "gm", "idb", True, True)
+        if t == 0:
+            pick("sg", (3, 0), 0, False)
         for k in range(12, 16):
             compare(k)
-        ts("cc", (2, 0), 9.0, None, A.is_ge)
-        tt((4, 2), "cc", (4, 0), A.mult)
         tt("omv", "mv", (1, 1), A.mult)
+        ts("cc", (2, 0), 9.0, None, A.is_ge)
+        tt("v1", "q1", (0, 1), A.is_equal)
+        pick("sg", (3, 0), 1, False)
+        tt((4, 2), "cc", (4, 0), A.mult)
+        tt((3, 1), "cc", (3, 0), A.mult)
         tt("nn", "nb", (4, 2), A.add)
-        dg = diag("sg", (3, 0), False)
+        tt("uw", "af", (3, 1), A.add)
         if not last:
             tt("nh", "nn", (1, 1), A.mult)
             for r in range(16):
                 mm((T.ps2[0:8, 128 + r:256:16], "ps2_1", 2), (T.nh[:, r:128:16], "nh"), (T.bo[:, 0:128:16], "bo"), True, True)
-            op("v", lambda: g.vector.tensor_copy(T.nxt[:, :].indirect(jl), T.nn[:, :]), ["nn", jk], ["nxt"])
-            op("v", lambda: g.vector.tensor_copy(T.jt8[:, :], T.ps2[0:8, 128:256]), ["ps2_1"], ["jt8"], (2,))
-        next(dg)
-        if not last:
-            mm(P((2, 2), 0, 8), "jt8", (T.idb[0:8, 0:8], "idb"), True, True)
-        next(dg)
-        if not last:
-            op("v", lambda: g.vector.tensor_scalar(lst("jl", t + 1), T.ps2[:, 256:264], 192.0, None, A.add), ["ps2_2"], ["jl%d" % (t + 1)], (2,))
-            limits(t + 1)
-            next_lists(t + 1)
-        tt((3, 1), "cc", (3, 0), A.mult)
-        tt("uw", "af", (3, 1), A.add)
         ts((3, 2), "uw", 1792.0, -1792.0, A.is_ge, A.mult)
+        if not last:
+            op("v", lambda: g.vector.tensor_copy(T.nxt[:, :].indirect(jl), T.nn[:, :]), ["nn", jk], ["nxt"])
         tt((3, 3), "uw", (3, 2), A.add)
         tt("uh", "uw", (3, 2), A.add)
+        if not last:
+            op("v", lambda: g.vector.tensor_copy(T.jt8[:, :], T.ps2[0:8, 128:256]), ["ps2_1"], ["jt8"], (2,))
+            mm(P((2, 2), 0, 8), "jt8", (T.idb[0:8, 0:8], "idb"), True, True)
         tt("e0", MN[0], (3, 3), A.is_equal)
         tt("e1", MN[1], (3, 3), A.is_equal)
         tt("e2", MN[2], (3, 3), A.is_equal)
-        o = P((5, 0))
-        mm(o, "idb", "e0", True, False)
-        mm(o, "idb", "e1", False, False)
-        mm(o, "idb", "e2", False, True)
+        o = P((5, 3))
+        mm(o, "id4m", "ones", True, False)
+        for x in ("e0", "e1", "e2"):
+            mm(o, "idn4m", x, False, x == "e2")
+        if not last:
+            op("v", lambda: g.vector.tensor_scalar(lst("jl", t + 1), T.ps2[:, 256:264], 192.0, None, A.add), ["ps2_2"], ["jl%d" % (t + 1)], (2,))
         tt("um", "mv", (3, 3), A.subtract)
+        if not last:
+            next_lists(t + 1)
+        ts("hit", (5, 3), 1.0, None, A.is_lt)
         tt((3, 1), "um", (1, 1), A.mult)
-        ts("hit", (5, 0), 1.0, None, A.min)
-        tt((3, 2), "hit", (3, 1), A.mult)
-        tt("vh", "omv", (3, 2), A.subtract)
         tt("hh", "hit", (1, 1), A.mult)
+        tt((3, 2), "hit", (3, 1), A.mult)
+        tt((0, 3), "q2", (5, 3), A.max)
+        tt("vh", "omv", (3, 2), A.subtract)
+        gv = "give%d" % t
+        if not last:
+            op("v", lambda: g.vector.tensor_copy(T.tool[:, :].indirect(jl), T.uh[:, :]), ["uh", jk], ["tool"])
+        tt(gv, "qv", (0, 3), A.min)
+        for b in range(2):
+            full = (T["ps%d" % (6 + b)][:, :], "ps%d" % (6 + b), 6 + b)
+            for q in range(4):
+                gg = 4 * b + q
+                mm((T["ps%d" % (6 + b)][:, 128 * q:128 * q + 128], "ps%d" % (6 + b), 6 + b), (T.gs[:, 128 * gg:128 * gg + 128], "gs"), "vh", False, False)
+            mm(full, "vh", (T.gsn[:, 512 * b:512 * b + 512], "gsn"), False, True)
+        mm(P((2, 2)), "bo", "hh", True, True)
+        o = P((1, 2), 0, 8)
+        for r in range(16):
+            mm(o, (T.eph[:, 16 - r:144 - r], "eph"), (T.vh[:, r:128:16], "vh"), r == 0, r == 15)
         o = P((5, 1))
         mm(o, "id15", "e0", True, False)
         mm(o, "id05", "v0", False, True)
@@ -331,83 +364,67 @@ def rank_program(g, core, T, topo):
         mm(o, "id15", "e1", True, False)
         mm(o, "idn15", "e0", False, False)
         mm(o, "id05", "v1", False, True)
-        for b in range(2):
-            full = (T["ps%d" % (6 + b)][:, :], "ps%d" % (6 + b), 6 + b)
-            for q in range(4):
-                gg = 4 * b + q
-                mm((T["ps%d" % (6 + b)][:, 128 * q:128 * q + 128], "ps%d" % (6 + b), 6 + b), (T.gs[:, 128 * gg:128 * gg + 128], "gs"), "vh", False, False)
-            mm(full, "vh", (T.gsn[:, 512 * b:512 * b + 512], "gsn"), False, True)
-            if b == 0:
-                mm(P((2, 2)), "bo", "hh", True, True)
-        o = P((1, 2), 0, 8)
-        for r in range(16):
-            mm(o, (T.eph[:, 16 - r:144 - r], "eph"), (T.vh[:, r:128:16], "vh"), r == 0, r == 15)
+        out = gv
+        if not last:
+            nexts(1)
+        else:
+            ts("gcl", gv, NOIDX, None, A.bitwise_and)
+            ts("gmm", gv, MSK, None, A.bitwise_and)
+            tt("gsum", "gcl", "gmm", A.add)
+        act("shf", (2, 2), IDN, extra=["rt8"], scale=T.rt8[:, t:t + 1], bias=-8.0)
+        if not last:
+            tool_lists(t + 1)
+            limits(t + 1)
+
+        def reduce(gg):
+            b, q = 6 + gg // 4, gg % 4
+            op("v", lambda: g.vector.tensor_reduce(T.dm[:, gg:gg + 1], T["ps%d" % b][:, 128 * q:128 * q + 128], AxisListType.X, A.min, apply_absolute_value=True),
+               ["ps%d" % b], ["dm%d" % gg], (b,))
+
+        for gg in range(4):
+            reduce(gg)
+        if last:
+            ts("gout", "gsum", 0.5, None, A.mult)
+            out = "gout"
+        wait("g", deps("g", [out], (), ()))
+        g.remote_dma(T["land%d" % t][:, :], T[out][:, :], T.sem["a%d" % t], T.sem.sent, pid, rid, mask)
+        for gg in range(4, 8):
+            reduce(gg)
+        vk, ok_ = "vl%d" % t, "ofl%d" % t
+        dmk = ["dm%d" % q for q in range(8)]
+        op("v", lambda: g.vector.tensor_copy(lst("vl", t), T.ps1[:, 256:264]), ["ps1_2"], [vk], (1,))
+        op("v", lambda: g.vector.tensor_copy(T.vlf[:, :], T.ps1[:, 256:264]), ["ps1_2"], ["vlf"], (1,))
+        op("v", lambda: g.vector.tensor_tensor(T.dup[:, :], T.dm[:, :].indirect(T.kg[:, :]), T.rm[:, :], A.is_equal), dmk + ["kg", "rm"], ["dup"])
+        mm((T.ps2[:, 384:392], "ps2_3", 2), "dup", "rc", True, True)
         for i in range(2):
             o = P((4, 2 + i))
             mm(o, "id8k", "nn", True, False)
             mm(o, "idh", "uh", False, False)
             mm(o, ("id4k", "id2k")[i], ("c385", "c769")[i], False, True)
-
-        def pockets(last=last):
-            tt("s0", "hit", (5, 1), A.is_lt)
-            tt("s1", "hit", (5, 2), A.is_lt)
-            tt((0, 0), "q0", (4, 2), A.subtract)
-            tt((0, 1), "q1", (4, 3), A.subtract)
-            tt((0, 0), "s0", (0, 0), A.mult)
-            tt((0, 1), "s1", (0, 1), A.mult)
-            tt("q0", "q0", (0, 0), A.subtract)
-            tt("q1", "q1", (0, 1), A.subtract)
-            ts("m0", "q0", MSK, None, A.bitwise_and)
-            ts("m1", "q1", MSK, None, A.bitwise_and)
-            MN[0], MN[1] = "m0", "m1"
-            if not last:
-                tt((0, 0), "q0", "q1", A.max)
-
-        late.append(pockets)
-
-        act("shf", (2, 2), IDN, extra=["rt8"], scale=T.rt8[:, t:t + 1], bias=-8.0)
-        gv = "give%d" % t
-        if not last:
-            nexts(1)
-            op("v", lambda: g.vector.tensor_copy(T.tool[:, :].indirect(jl), T.uh[:, :]), ["uh", jk], ["tool"])
-        tt((0, 3), "hit", (0, 2), A.mult)
-        tt(gv, "qv", (0, 3), A.add)
-        if not last:
-            tool_lists(t + 1)
-            out = gv
-        else:
-            ts("gcl", gv, NOIDX, None, A.bitwise_and)
-            ts("gmm", gv, MSK, None, A.bitwise_and)
-            tt("gsum", "gcl", "gmm", A.add)
-            ts("gout", "gsum", 0.5, None, A.mult)
-            out = "gout"
-        wait("g", deps("g", [out], (), ()))
-        g.remote_dma(T["land%d" % t][:, :], T[out][:, :], T.sem["a%d" % t], T.sem.sent, pid, rid, mask)
-        for gg in range(8):
-            b, q = 6 + gg // 4, gg % 4
-            op("v", lambda: g.vector.tensor_reduce(T.dm[:, gg:gg + 1], T["ps%d" % b][:, 128 * q:128 * q + 128], AxisListType.X, A.min, apply_absolute_value=True),
-               ["ps%d" % b], ["dm%d" % gg], (b,))
-        vk, ok_ = "vl%d" % t, "ofl%d" % t
-        dmk = ["dm%d" % q for q in range(8)]
-        op("v", lambda: g.vector.tensor_tensor(T.dup[:, :], T.dm[:, :].indirect(T.kg[:, :]), T.rm[:, :], A.is_equal), dmk + ["kg", "rm"], ["dup"])
-        op("v", lambda: g.vector.tensor_copy(lst("vl", t), T.ps1[:, 256:264]), ["ps1_2"], [vk], (1,))
-        op("v", lambda: g.vector.tensor_copy(T.vlf[:, :], T.ps1[:, 256:264]), ["ps1_2"], ["vlf"], (1,))
-        mm((T.ps2[:, 384:392], "ps2_3", 2), "dup", "rc", True, True)
+        tt("s0", "hit", (5, 1), A.is_lt)
+        tt("s1", "hit", (5, 2), A.is_lt)
         tt("yy", (T.xt[:, 0:W].indirect(lst("vl", t)), "xt"), "shf", A.add, extra=[vk])
         op("v", lambda: g.vector.tensor_tensor(T.off[:, :], T.vlf[:, :], T.ps2[:, 384:392], A.max), ["vlf", "ps2_3"], ["off"], (2,))
+        tt((0, 0), "q0", (4, 2), A.subtract)
         ts("yc", "yy", 0.0, 255.0, A.max, A.min)
         op("v", lambda: g.vector.tensor_copy(lst("ofl", t), T.off[:, :]), ["off"], [ok_])
+        tt((0, 1), "q1", (4, 3), A.subtract)
         op("v", lambda: g.vector.tensor_copy(T.xt[:, :].indirect(lst("ofl", t)), T.yc[:, :]), ["yc", ok_], ["xt"])
+        tt((0, 0), "s0", (0, 0), A.mult)
+        tt((0, 1), "s1", (0, 1), A.mult)
         if last:
             dma("y", T.yx[:, :], T.xt[:, 0:W], "ox", r=["xt"])
-            pockets()
+            g.scalar.wait_ge(T.sem.a2, nrec)
+            g.scalar.dma_start(T.yp[:, 256:384], T.land2[:, :]).then_inc(T.sem.oq, 16)
+            for i in range(2):
+                tt("q%d" % i, "q%d" % i, (0, i), A.subtract)
+            for i in range(2):
+                ts("m%d" % i, "q%d" % i, MSK, None, A.bitwise_and)
             for i in range(2):
                 tt((T.ys[:, 128 * i:128 * i + 128], "ys%d" % i), "q%d" % i, "m%d" % i, A.add)
             for i in range(2):
                 ts((T.yo[:, 128 * i:128 * i + 128], "yo%d" % i), (T.ys[:, 128 * i:128 * i + 128], "ys%d" % i), 0.5, -1024.0 * (2 - i), A.mult, A.add)
             dma("s", T.yp[:, 0:256], T.yo[:, :], "op", r=["yo0", "yo1"])
-    g.scalar.wait_ge(T.sem.a2, nrec)
-    g.scalar.dma_start(T.yp[:, 256:384], T.land2[:, :]).then_inc(T.sem.oq, 16)
     for sem in ("sv", "ss", "sp", "sg"):
         g.wait_ge(T.sem[sem], cnt[sem])
     g.wait_ge(T.sem.sent, NT * len(topo.engines(core, nxt_core)))

from concourse.mybir import AluOpType, AxisListType, ActivationFunctionType

A = AluOpType
CPY = ActivationFunctionType.Copy
IDN = ActivationFunctionType.Identity
W, MA, J, NT = 1792, 128, 384, 3
XV = (112, 40, 40)
C1 = 8

_B, _H, _F, _I, _U = "bfloat16", "float16", "float32", "int32", "uint16"
SCRATCH = {}
for _names, _w, _d in (
        ("sdt", W, _B), ("xt", W + MA, _B), ("lmt nxt", J, _B), ("rtb", NT, _B), ("rt8", NT, _F),
        ("jtt pkt tint nint mall", J, _I), ("jmt kgi", 8, _I), ("tool", J, _F), ("jl vl ofl", 8 * NT, _U), ("al nl", 128, _U),
        ("xa sg ng ov fd", 2048, _B), ("gm", 128, _B), ("af pre key uw um gout gsum msk rm land2", 128, _F),
        ("lg nb cc nn nh e0 e1 e2 hit hh v0 v1 s0 s1 shf yy yc", 128, _B), ("uh omv vh dup", 128, _H),
        ("q0 q1 q2 qv m0 m1 m2 mv give0 give1 give2 gcl gmm land0 land1 iot pmi", 128, _I),
        ("dm vlf off rcf", 8, _F), ("yo ys", 256, _F), ("zer tri", 512, _B), ("rc", 8, _H), ("kg k15", 8, _U), ("e16", 8, _B),
        ("ones id4m idn4m idb idn id15 idn15 id05 id8k bt bo tie", 128, _B), ("idh id4k id2k c385 c769", 128, _H),
        ("ep", 160, _B), ("eph", 160, _H), ("gs gsn", 1024, _H)):
    for _n in _names.split():
        SCRATCH[_n] = ("sbuf", [128, _w], _d)
SCRATCH["jt8"] = ("sbuf", [8, 128], _B)
for _k in range(8):
    SCRATCH["ps%d" % _k] = ("psum", [128, 512], _F)
SEMAPHORES = ["sv", "ss", "sp", "sg", "ljm", "ljt", "llm", "lpk", "lrt", "lxw", "lsd", "a0", "a1", "a2", "sent", "ox", "op", "oq"]
MSK, NOIDX = 2047, 4188159


def rank_program(g, core, T, topo):
    rank = T.rank_of(core)
    if rank is None:
        return
    nxt_core = T.cores[(rank + 1) % len(T.cores)]
    prv_core = T.cores[(rank - 1) % len(T.cores)]
    rid, pid = topo.addr(nxt_core, core)
    mask = topo.mask(core, nxt_core)
    nrec = len(topo.engines(prv_core, core))

    ENG = {"v": g.vector, "s": g.scalar, "p": g.tensor, "g": g, "y": g.sync}
    OWN = {"v": "sv", "s": "ss", "p": "sp", "g": "sg"}
    cnt = {"sv": 0, "ss": 0, "sp": 0, "sg": 0}
    clk = {e: {} for e in ENG}
    snap = {}
    wr, rd, bk = {}, {}, {}

    def wait(e, toks):
        for tk in sorted(toks, key=lambda q: (-len(snap[q]), q)):
            sem, val = tk
            if clk[e].get(sem, 0) >= val:
                continue
            if any(o != tk and snap[o].get(sem, 0) >= val and clk[e].get(o[0], 0) < o[1] for o in toks):
                continue
            ENG[e].wait_ge(T.sem[sem], val)
            for a, b in snap[tk].items():
                if clk[e].get(a, 0) < b:
                    clk[e][a] = b

    def deps(e, r, w, banks):
        toks = set()
        for k in r:
            if k in wr:
                toks.add(wr[k][1])
        for k in w:
            if k in wr:
                toks.add(wr[k][1])
            for e2, tk in rd.get(k, {}).items():
                if e2 != e:
                    toks.add(tk)
        for b in banks:
            for e2, tk in bk.get(b, {}).items():
                if e2 != e:
                    toks.add(tk)
        if e == "p":
            toks = {q for q in toks if q[0] != "sp"}
        return toks

    def note(e, tk, r, w, banks):
        s = dict(clk[e])
        if s.get(tk[0], 0) < tk[1]:
            s[tk[0]] = tk[1]
        snap[tk] = s
        for k in w:
            wr[k] = (e, tk)
            rd[k] = {}
        for k in r:
            rd.setdefault(k, {})[e] = tk
        for b in banks:
            bk.setdefault(b, {})[e] = tk

    def op(e, call, r=(), w=(), b=()):
        wait(e, deps(e, r, w, b))
        ins = call()
        sem = OWN[e]
        cnt[sem] += 1
        ins.then_inc(T.sem[sem], 1)
        note(e, (sem, cnt[sem]), r, w, b)

    def dma(e, out, in_, sem, r=(), w=()):
        wait(e, deps(e, r, w, ()))
        ENG[e].dma_start(out, in_).then_inc(T.sem[sem], 16)
        note(e, (sem, 16), r, w, ())

    def res(x):
        if isinstance(x, str):
            return T[x][:, :], x, ()
        if isinstance(x[0], int):
            return T["ps%d" % x[0]][:, 128 * x[1]:128 * x[1] + 128], "ps%d_%d" % x, (x[0],)
        return x[0], x[1], ()

    def tt(out, a, b, o, extra=()):
        (oa, ok, ob), (aa, ak, ab), (ba, bkk, bb) = res(out), res(a), res(b)
        op("v", lambda: g.vector.tensor_tensor(oa, aa, ba, o), [ak, bkk] + list(extra), [ok], set(ob) | set(ab) | set(bb))

    def ts(out, a, s1, s2, o0, o1=None, extra=()):
        (oa, ok, ob), (aa, ak, ab) = res(out), res(a)
        if o1 is None:
            f = lambda: g.vector.tensor_scalar(oa, aa, s1, None, o0)
        else:
            f = lambda: g.vector.tensor_scalar(oa, aa, s1, s2, o0, o1)
        op("v", f, [ak] + list(extra), [ok], set(ob) | set(ab))

    def cp(out, a, extra=()):
        (oa, ok, ob), (aa, ak, ab) = res(out), res(a)
        op("v", lambda: g.vector.tensor_copy(oa, aa), [ak] + list(extra), [ok], set(ob) | set(ab))

    def act(out, a, func=CPY, extra=(), **kw):
        (oa, ok, ob), (aa, ak, ab) = res(out), res(a)
        op("s", lambda: g.scalar.activation(oa, aa, func, **kw), [ak] + list(extra), [ok], set(ob) | set(ab))

    def mm(out, l, r, st, sp):
        (la, lk, _x), (ra, rk, _y) = res(l), res(r)
        op("p", lambda: g.tensor.matmul(out[0], la, ra, st, sp), [lk, rk], [out[1]], (out[2],))

    def P(p, a=0, b=128, step=1):
        base = 128 * p[1]
        return (T["ps%d" % p[0]][:, base + a:base + b:step], "ps%d_%d" % p, p[0])

    def lst(nm, t):
        return T[nm][:, 8 * t:8 * t + 8]

    dma("y", T.jmt[:, :], T.jm[:, :], "ljm", w=["jmt"])
    dma("s", T.jtt[:, :], T.jt[:, :], "ljt", w=["jtt"])
    dma("y", T.xt[:, 0:W], T.xw[:, :], "lxw", w=["xt"])
    dma("y", T.lmt[:, :], T.lm[:, :], "llm", w=["lmt"])
    dma("s", T.sdt[:, :], T.sd[:, :], "lsd", w=["sdt"])
    dma("y", T.rtb[:, :], T.rt[:, :], "lrt", w=["rtb"])
    dma("y", T.pkt[:, :], T.pk[:, :], "lpk", w=["pkt"])

    def fill(ap, key, c):
        op("v", lambda: g.vector.memset(ap, c), (), [key])

    def asel(out, in_, pat, cmp_, f, base, cm):
        op("g", lambda: g.affine_select(T[out][:, :], T[in_][:, :], pat, cmp_, f, base, cm), [in_], [out])

    fill(T.ones[:, :], "ones", 1.0)
    fill(T.zer[:, :], "zer", 0.0)
    fill(T.fd[:, :], "fd", 0.0)
    asel("bt", "ones", [[-16, 8], [0, 16]], A.is_ge, 0.0, 0, 1)
    asel("bo", "bt", [[16, 8], [0, 16]], A.is_ge, 0.0, 15, -1)
    asel("idb", "ones", [[-1, 128]], A.is_equal, 0.0, 0, 1)
    op("g", lambda: g.iota(T.tie[:, :], [[0, 8], [-1, 16]], 15, 0, allow_small_or_imprecise_dtypes=True), (), ["tie"])
    op("g", lambda: g.iota(T.kgi[:, :], [[1, 8]], 0, 0), (), ["kgi"])
    op("g", lambda: g.iota(T.iot[:, :], [[-1, 128]], 128, 1), (), ["iot"])
    op("g", lambda: g.iota(T.rcf[:, :], [[0, 8]], 1792, 1, allow_small_or_imprecise_dtypes=True), (), ["rcf"])
    asel("tri", "zer", [[0, 4], [-1, 128]], A.is_ge, 4096.0, -1, 1)
    fill(T.ep[:, :], "ep", 0.0)
    for k in range(16):
        op("s", lambda: g.scalar.activation(T.fd[:, 129 * k:128 * k + 128:16], T.idb[:, k:128:16], CPY), ["idb"] + (["fd"] if k == 0 else []), ["fd%d" % k])
    for nm, c in (("idn", -1.0), ("id15", 1.5), ("idn15", -1.5), ("id05", 0.5), ("id8k", 8192.0), ("id4m", 4194304.0), ("idn4m", -4194304.0)):
        act(nm, "idb", scale=c)
    ts("c385", "ones", 385.0, None, A.mult)
    ts("c769", "ones", 769.0, None, A.mult)
    op("v", lambda: g.vector.tensor_copy(T.ep[:, 16:144:16], T.bo[:, 0:128:16]), ["bo"], ["ep"])
    op("v", lambda: g.vector.tensor_scalar(T.e16[:, :], T.bo[:, 0:128:16], 16.0, None, A.mult), ["bo"], ["e16"])
    for q in range(8):
        op("v", lambda: g.vector.tensor_scalar(T.gs[:, 128 * q:128 * q + 128], T.ones[:, :], T.bo[:, 16 * q:16 * q + 1], None, A.mult), ["ones", "bo"], ["gs"] if q == 7 else ["gs_%d" % q])
    ts("msk", "tie", 15.0, None, A.is_lt)
    op("v", lambda: g.vector.tensor_scalar(T.k15[:, :], T.kgi[:, :], 16.0, 15.0, A.mult, A.add), ["kgi"], ["k15"])

    op("v", lambda: g.vector.tensor_copy(lst("jl", 0), T.jmt[:, :]), ["jmt"], ["jl0"])
    ts("nint", "jtt", 12, None, A.logical_shift_right)
    ts("tint", "jtt", 4095, None, A.bitwise_and)
    ts("nxt", "nint", -192.0, None, A.add)
    cp("tool", "tint")

    def nexts(h):
        act((T.ng[:, 1024 * h:1024 * h + 1024], "ng%d" % h), (T.nxt[:, :].indirect(T.nl[:, 64 * h:64 * h + 64]), "nxt"), extra=["nl"])

    def sisters(h):
        act((T.sg[:, 1024 * h:1024 * h + 1024], "sg%d" % h), (T.sdt[:, :].indirect(T.al[:, 64 * h:64 * h + 64]), "sdt"), extra=["al"])

    def next_lists(t):
        jk, jl = "jl%d" % t, lst("jl", t)
        ts("nl", (T.nxt[:, :].indirect(jl), "nxt"), 192.0, None, A.add, extra=[jk])
        act("nb", (T.nxt[:, :].indirect(jl), "nxt"), extra=[jk])
        nexts(0)

    def tool_lists(t):
        jk, jl = "jl%d" % t, lst("jl", t)
        cp("al", (T.tool[:, :].indirect(jl), "tool"), extra=[jk])
        act("af", (T.tool[:, :].indirect(jl), "tool"), extra=[jk])

    def limits(t):
        act("lg", (T.lmt[:, :].indirect(lst("jl", t)), "lmt"), extra=["jl%d" % t])

    def pick(src, piece, h, first):
        o = P(piece, 64 * h, 64 * h + 64)
        if first:
            mm(o, "idn", (T.nb[:, 64 * h:64 * h + 64], "nb"), True, False)
        for k in range(16):
            mm(o, (T.fd[:, 128 * k:128 * k + 128], "fd%d" % k), (T[src][:, 1024 * h + k:1024 * h + 1024:16], "%s%d" % (src, h)),
               k == 0 and not first, k == 15)

    next_lists(0)
    tool_lists(0)
    nexts(1)
    limits(0)
    ts("gsn", "gs", -1.0, None, A.mult, extra=["gs_%d" % q for q in range(7)])
    cp("idh", "idb")
    cp("eph", "ep")
    ts("id4k", "idb", 4096.0, None, A.mult)
    ts("id2k", "idb", 2048.0, None, A.mult)
    ts("pmi", "iot", 15, None, A.bitwise_and)
    op("v", lambda: g.vector.tensor_tensor(T.rc[:, :], T.rcf[:, :], T.bo[:, 0:128:16], A.mult), ["rcf", "bo"], ["rc"])
    cp("kg", "kgi")
    ts("rm", "pmi", 0.0, -1.0, A.is_equal, A.add)

    MN = [(T.mall[:, 0:128], "mall"), (T.mall[:, 128:256], "mall"), (T.mall[:, 256:384], "mall")]

    def first_pockets():
        ts("mall", "pkt", 4095, None, A.bitwise_and)
        for i in range(3):
            ts((0, i), (T.pkt[:, 128 * i:128 * i + 128], "pkt"), 2.0, 2048.0 * (2 - i), A.mult, A.add)
        for i in range(3):
            tt("q%d" % i, (0, i), MN[i], A.subtract)
        tt((0, 0), "q0", "q1", A.max)

    for t in range(NT):
        last = t == NT - 1
        jk, jl = "jl%d" % t, lst("jl", t)
        xv = XV[t]
        if t:
            sisters(0)
        op("v", lambda: g.vector.tensor_copy(T.xa[:, 0:16 * xv], T.xt[:, 0:W].indirect(T.al[:, 0:xv])), ["xt", "al"], ["xa0"])
        op("s", lambda: g.scalar.activation(T.xa[:, 16 * xv:2048], T.xt[:, 0:W].indirect(T.al[:, xv:128]), CPY), ["xt", "al"], ["xa1"])
        if t == 0:
            sisters(0)
        sisters(1)
        pick("ng", (4, 0), 0, True)
        pick("ng", (4, 0), 1, True)
        mm(P((4, 1)), "idb", "lg", True, True)
        if t:
            pick("sg", (3, 0), 0, False)
        for b in range(2):
            mm((T["ps%d" % (6 + b)][:, :], "ps%d" % (6 + b), 6 + b), "idb", "tri", True, False)
        mm(P((1, 0)), "idb", "tie", True, False)
        for k in range(16):
            o = P((1, 0), k, 128, 16)
            op("p", lambda: g.tensor.matmul(o[0], T.xa[:, k:2048:16], T.e16[:, :], False, k == 15), ["xa0", "xa1", "e16"], [o[1]], (1,))

        def beginning():
            if t == 0:
                first_pockets()
                ts("rt8", "rtb", 8.0, None, A.add)
            else:
                tt("q0", "q0", (0, 0), A.subtract)
                tt("q1", "q1", (0, 1), A.subtract)
                ld = "land%d" % (t - 1)
                tk = ("a%d" % (t - 1), nrec)
                snap[tk] = {tk[0]: nrec}
                wr[ld] = ("r", tk)
                ts("m0", "q0", MSK, None, A.bitwise_and)
                ts("m1", "q1", MSK, None, A.bitwise_and)
                tt((0, 0), "q0", "q1", A.max)
                ts("q2", ld, NOIDX, None, A.bitwise_and)
                MN[0], MN[1], MN[2] = "m0", "m1", "m2"
                ts("m2", ld, MSK, None, A.bitwise_and)
            tt((0, 1), (0, 0), "q2", A.max)
            tt("qv", (0, 0), "q2", A.max)
            tt("v0", "q0", (0, 1), A.is_equal)
            ts("mv", "qv", MSK, None, A.bitwise_and)

        if t:
            beginning()

        def compare(k):
            op("v", lambda: g.vector.tensor_tensor(T.ov[:, 128 * k:128 * k + 128], T.xa[:, k:2048:16], T.ps4[:, 128:256], A.is_gt),
               ["xa0", "xa1", "ps4_1"], ["ov%d" % k], (4,))
            mm(P((2, 0)), (T.ep[:, 16 - k:144 - k], "ep"), (T.ov[:, 128 * k:128 * k + 128], "ov%d" % k), k == 0, k == 15)

        for k in range(C1):
            compare(k)
        op("v", lambda: g.vector.tensor_tensor_scan(T.pre[:, :], T.msk[:, :], T.ps1[:, 0:128], 0.0, A.mult, A.max), ["msk", "ps1_0"], ["pre"], (1,))
        cp("key", (1, 0))
        compare(C1)
        compare(C1 + 1)
        tt("gm", (T.pre[:, :].indirect(T.k15[:, :]), "pre"), "key", A.is_equal, extra=["k15"])
        for k in range(C1 + 2, 12):
            compare(k)
        if t == 0:
            beginning()
        mm(P((1, 1)), "gm", "idb", True, True)
        if t == 0:
            pick("sg", (3, 0), 0, False)
        for k in range(12, 16):
            compare(k)
        tt("omv", "mv", (1, 1), A.mult)
        ts("cc", (2, 0), 9.0, None, A.is_ge)
        tt("v1", "q1", (0, 1), A.is_equal)
        pick("sg", (3, 0), 1, False)
        tt((4, 2), "cc", (4, 0), A.mult)
        tt((3, 1), "cc", (3, 0), A.mult)
        tt("nn", "nb", (4, 2), A.add)
        tt("uw", "af", (3, 1), A.add)
        if not last:
            tt("nh", "nn", (1, 1), A.mult)
            for r in range(16):
                mm((T.ps2[0:8, 128 + r:256:16], "ps2_1", 2), (T.nh[:, r:128:16], "nh"), (T.bo[:, 0:128:16], "bo"), True, True)
        ts((3, 2), "uw", 1792.0, -1792.0, A.is_ge, A.mult)
        if not last:
            op("v", lambda: g.vector.tensor_copy(T.nxt[:, :].indirect(jl), T.nn[:, :]), ["nn", jk], ["nxt"])
        tt((3, 3), "uw", (3, 2), A.add)
        tt("uh", "uw", (3, 2), A.add)
        if not last:
            op("v", lambda: g.vector.tensor_copy(T.jt8[:, :], T.ps2[0:8, 128:256]), ["ps2_1"], ["jt8"], (2,))
            mm(P((2, 2), 0, 8), "jt8", (T.idb[0:8, 0:8], "idb"), True, True)
        tt("e0", MN[0], (3, 3), A.is_equal)
        tt("e1", MN[1], (3, 3), A.is_equal)
        tt("e2", MN[2], (3, 3), A.is_equal)
        o = P((5, 3))
        mm(o, "id4m", "ones", True, False)
        for x in ("e0", "e1", "e2"):
            mm(o, "idn4m", x, False, x == "e2")
        if not last:
            op("v", lambda: g.vector.tensor_scalar(lst("jl", t + 1), T.ps2[:, 256:264], 192.0, None, A.add), ["ps2_2"], ["jl%d" % (t + 1)], (2,))
        tt("um", "mv", (3, 3), A.subtract)
        if not last:
            next_lists(t + 1)
        ts("hit", (5, 3), 1.0, None, A.is_lt)
        tt((3, 1), "um", (1, 1), A.mult)
        tt("hh", "hit", (1, 1), A.mult)
        tt((3, 2), "hit", (3, 1), A.mult)
        tt((0, 3), "q2", (5, 3), A.max)
        tt("vh", "omv", (3, 2), A.subtract)
        gv = "give%d" % t
        if not last:
            op("v", lambda: g.vector.tensor_copy(T.tool[:, :].indirect(jl), T.uh[:, :]), ["uh", jk], ["tool"])
        tt(gv, "qv", (0, 3), A.min)
        for b in range(2):
            full = (T["ps%d" % (6 + b)][:, :], "ps%d" % (6 + b), 6 + b)
            for q in range(4):
                gg = 4 * b + q
                mm((T["ps%d" % (6 + b)][:, 128 * q:128 * q + 128], "ps%d" % (6 + b), 6 + b), (T.gs[:, 128 * gg:128 * gg + 128], "gs"), "vh", False, False)
            mm(full, "vh", (T.gsn[:, 512 * b:512 * b + 512], "gsn"), False, True)
        mm(P((2, 2)), "bo", "hh", True, True)
        o = P((1, 2), 0, 8)
        for r in range(16):
            mm(o, (T.eph[:, 16 - r:144 - r], "eph"), (T.vh[:, r:128:16], "vh"), r == 0, r == 15)
        o = P((5, 1))
        mm(o, "id15", "e0", True, False)
        mm(o, "id05", "v0", False, True)
        o = P((5, 2))
        mm(o, "id15", "e1", True, False)
        mm(o, "idn15", "e0", False, False)
        mm(o, "id05", "v1", False, True)
        out = gv
        if not last:
            nexts(1)
        else:
            ts("gcl", gv, NOIDX, None, A.bitwise_and)
            ts("gmm", gv, MSK, None, A.bitwise_and)
            tt("gsum", "gcl", "gmm", A.add)
        act("shf", (2, 2), IDN, extra=["rt8"], scale=T.rt8[:, t:t + 1], bias=-8.0)
        if not last:
            tool_lists(t + 1)
            limits(t + 1)

        def reduce(gg):
            b, q = 6 + gg // 4, gg % 4
            op("v", lambda: g.vector.tensor_reduce(T.dm[:, gg:gg + 1], T["ps%d" % b][:, 128 * q:128 * q + 128], AxisListType.X, A.min, apply_absolute_value=True),
               ["ps%d" % b], ["dm%d" % gg], (b,))

        for gg in range(4):
            reduce(gg)
        if last:
            ts("gout", "gsum", 0.5, None, A.mult)
            out = "gout"
        wait("g", deps("g", [out], (), ()))
        g.remote_dma(T["land%d" % t][:, :], T[out][:, :], T.sem["a%d" % t], T.sem.sent, pid, rid, mask)
        for gg in range(4, 8):
            reduce(gg)
        vk, ok_ = "vl%d" % t, "ofl%d" % t
        dmk = ["dm%d" % q for q in range(8)]
        op("v", lambda: g.vector.tensor_copy(lst("vl", t), T.ps1[:, 256:264]), ["ps1_2"], [vk], (1,))
        op("v", lambda: g.vector.tensor_copy(T.vlf[:, :], T.ps1[:, 256:264]), ["ps1_2"], ["vlf"], (1,))
        op("v", lambda: g.vector.tensor_tensor(T.dup[:, :], T.dm[:, :].indirect(T.kg[:, :]), T.rm[:, :], A.is_equal), dmk + ["kg", "rm"], ["dup"])
        mm((T.ps2[:, 384:392], "ps2_3", 2), "dup", "rc", True, True)
        for i in range(2):
            o = P((4, 2 + i))
            mm(o, "id8k", "nn", True, False)
            mm(o, "idh", "uh", False, False)
            mm(o, ("id4k", "id2k")[i], ("c385", "c769")[i], False, True)
        tt("s0", "hit", (5, 1), A.is_lt)
        tt("s1", "hit", (5, 2), A.is_lt)
        tt("yy", (T.xt[:, 0:W].indirect(lst("vl", t)), "xt"), "shf", A.add, extra=[vk])
        op("v", lambda: g.vector.tensor_tensor(T.off[:, :], T.vlf[:, :], T.ps2[:, 384:392], A.max), ["vlf", "ps2_3"], ["off"], (2,))
        tt((0, 0), "q0", (4, 2), A.subtract)
        ts("yc", "yy", 0.0, 255.0, A.max, A.min)
        op("v", lambda: g.vector.tensor_copy(lst("ofl", t), T.off[:, :]), ["off"], [ok_])
        tt((0, 1), "q1", (4, 3), A.subtract)
        op("v", lambda: g.vector.tensor_copy(T.xt[:, :].indirect(lst("ofl", t)), T.yc[:, :]), ["yc", ok_], ["xt"])
        tt((0, 0), "s0", (0, 0), A.mult)
        tt((0, 1), "s1", (0, 1), A.mult)
        if last:
            dma("y", T.yx[:, :], T.xt[:, 0:W], "ox", r=["xt"])
            g.scalar.wait_ge(T.sem.a2, nrec)
            g.scalar.dma_start(T.yp[:, 256:384], T.land2[:, :]).then_inc(T.sem.oq, 16)
            for i in range(2):
                tt("q%d" % i, "q%d" % i, (0, i), A.subtract)
            for i in range(2):
                ts("m%d" % i, "q%d" % i, MSK, None, A.bitwise_and)
            for i in range(2):
                tt((T.ys[:, 128 * i:128 * i + 128], "ys%d" % i), "q%d" % i, "m%d" % i, A.add)
            for i in range(2):
                ts((T.yo[:, 128 * i:128 * i + 128], "yo%d" % i), (T.ys[:, 128 * i:128 * i + 128], "ys%d" % i), 0.5, -1024.0 * (2 - i), A.mult, A.add)
            dma("s", T.yp[:, 0:256], T.yo[:, :], "op", r=["yo0", "yo1"])
    for sem in ("sv", "ss", "sp", "sg"):
        g.wait_ge(T.sem[sem], cnt[sem])
    g.wait_ge(T.sem.sent, NT * len(topo.engines(core, nxt_core)))
    for sem in ("ox", "op", "oq"):
        g.wait_ge(T.sem[sem], 16)
